import numpy as np
import ml_dtypes


def mxq(x, axis, fmt="e4m3"):
    dtype, down = {"e4m3": (ml_dtypes.float8_e4m3fn, 7), "e5m2": (ml_dtypes.float8_e5m2, 14)}[fmt]
    v = np.moveaxis(np.asarray(x, np.float32).astype(ml_dtypes.bfloat16).astype(np.float64), axis, -1)
    blocks = v.reshape(v.shape[:-1] + (-1, 32))
    amax = np.abs(blocks).max(-1, keepdims=True)
    byte = np.maximum(np.where(amax > 0, np.frexp(amax)[1] - 1 + 127, 0) - down, 1)
    scale = np.exp2(byte - 127.0)
    codes = (blocks / scale).astype(np.float32).astype(dtype).astype(np.float64)
    return np.moveaxis((codes * scale).reshape(v.shape), -1, axis)


WIDE = False


def mx_kscale(k):
    if not WIDE:
        return np.ones(k)
    levels = np.array([10, -10, 5, -5, 0])
    if k % 512:
        return np.exp2(np.random.permutation(np.resize(levels, k // 32))).repeat(32)
    a = np.empty((k // 512, 16))
    for p in range(k // 512):
        a[p, :8] = np.random.permutation(np.resize(levels, 8))
        for g in range(8):
            far = levels[np.abs(levels - a[p, g]) >= 10]
            a[p, g + 8] = far[np.random.randint(len(far))]
    return np.exp2(a.ravel()).repeat(32)


def f64(x):
    return np.asarray(x).astype(np.float64)


def striped(idx):
    return np.tile(idx.reshape(-1, 16).T, (8, 1)).astype(np.uint16)


def unstriped(offs):
    return offs[:16].T.reshape(-1).astype(np.int64)


def striped8(idx):
    return np.concatenate([x.reshape(-1, 16).T for x in idx]).astype(np.uint16)


def runs(offs, k):
    lists = np.stack([offs[16 * r : 16 * r + 16].T.reshape(-1) for r in range(8)]).astype(np.int64)
    return lists[np.arange(k) % 512 // 64]


def pack_weight(w):
    k, n = w.shape
    w = f64(np.asarray(w, np.float32).astype(ml_dtypes.bfloat16)).reshape(k // 32, 32, n)
    amax = np.abs(w).max(1)
    byte = np.clip(np.where(amax > 0, np.frexp(amax)[1] - 1 + 127 - 7, 1), 1, 254)
    scaled = (w * np.exp2(127.0 - byte)[:, None, :]).reshape(k, n).astype(np.float32)
    words = np.ascontiguousarray(scaled.reshape(k // 512, 128, 4, n).transpose(0, 1, 3, 2)).astype(ml_dtypes.float8_e4m3fn).view(np.uint8)
    return words, np.ascontiguousarray(byte.astype(np.uint8).reshape(k // 512, 16, n))


def unpack_weight(words, scales):
    g, p, n, _ = words.shape
    vals = np.ascontiguousarray(words).view(ml_dtypes.float8_e4m3fn).astype(np.float64) * np.repeat(np.exp2(scales.astype(np.float64) - 127.0), 8, axis=1)[..., None]
    return vals.transpose(0, 1, 3, 2).reshape(g * 512, n)


def sigmoid(v):
    return 1.0 / (1.0 + np.exp(-np.maximum(v, -700.0)))


K, T, S, N, H = 512, 2048, 512, 512, 512


def setup_inputs():
    n = np.random.standard_normal
    s = mx_kscale(K)[:, None]
    u = mx_kscale(H)
    packed_xT = pack_weight(n((K, T)) * s)
    return {
        "x_words": packed_xT[0],
        "x_scales": packed_xT[1],
        "w1": (n((K, H)) / np.sqrt(K) / s).astype(np.float32),
        "gn": (np.random.uniform(0.5, 1.5, (H, 1)) * u[:, None]).astype(np.float32),
        "w2": (n((H, N)) / np.sqrt(2 * H) / u[:, None]).astype(np.float32),
        "w3": (n((K, N)) / np.sqrt(2 * K) / s).astype(np.float32),
        "offs": striped(np.random.permutation(T)[:S]),
        "n1": striped8(np.stack([np.random.permutation(S) for _ in range(8)])),
        "n2": striped8(np.stack([np.random.permutation(S) for _ in range(8)])),
        "two": striped(np.random.permutation(T)[:S]),
        "n3": striped(np.random.permutation(S)),
    }


def reference(x_words, x_scales, w1, gn, w2, w3, offs, n1, n2, two, n3):
    xq = unpack_weight(x_words, x_scales)[:, unstriped(offs)]
    y = mxq(f64(w1), 0, "e4m3").T @ xq
    st = np.maximum(y, y[np.arange(H)[:, None], runs(n1, H)])
    z = f64(gn) * (np.minimum(st, st[np.arange(H)[:, None], runs(n2, H)]))
    x_two = unpack_weight(x_words, x_scales)[:, unstriped(two)]
    h = mxq(f64(w2), 0, "e4m3").T @ mxq(z, 0, "e4m3") + mxq(f64(w3), 0, "e4m3").T @ x_two
    return h * (sigmoid(h[:, unstriped(n3)]))

@@ -1,0 +1,210 @@
+from contextlib import ExitStack
+
+import concourse.mybir as mybir
+
+K, T, S, N, H = 512, 2048, 512, 512, 512
+FLOPS = 2 * S * (K * H + H * N + K * N)
+
+F32 = mybir.dt.float32
+BF16 = mybir.dt.bfloat16
+I32 = mybir.dt.int32
+U32 = mybir.dt.uint32
+U16 = mybir.dt.uint16
+U8 = mybir.dt.uint8
+FP8X4 = mybir.dt.float8_e4m3fn_x4
+ALU = mybir.AluOpType
+ACT = mybir.ActivationFunctionType
+
+P = 128
+PACK = 4
+GROUP = 16
+HALF = S // 2
+CHUNKS = (256, 128, 128)
+
+
+def tile_picked_mixinhopmngate_none_p_kernel(
+    tc, x_words, x_scales, w1, gn, w2, w3, offs, n1, n2, two, n3, out
+):
+    nc = tc.nc
+    with ExitStack() as ctx:
+        keep = ctx.enter_context(tc.tile_pool(name="keep", bufs=1))
+        psum = ctx.enter_context(tc.psum_pool(name="psum", bufs=1))
+
+        def load_list(name, dram):
+            tile = keep.tile([P, S // GROUP], U16, name=name)
+            nc.sync.dma_start(tile[:], dram)
+            return tile
+
+        def entries(tile, start, count):
+            return tile[:, start // GROUP : (start + count) // GROUP]
+
+        def load_weight(name, dram, c0, width):
+            tile = keep.tile([P, PACK, width], F32, name=name)
+            nc.sync.dma_start(tile[:], dram.rearrange("(p j) c -> p j c", j=PACK)[:, :, c0 : c0 + width])
+            return tile
+
+        offs_sb = load_list("offs_sb", offs)
+        table_words = keep.tile([P, T], I32, name="table_words")
+        nc.sync.dma_start(table_words[:], x_words[0].rearrange("p n t -> p (n t)").bitcast(I32))
+        table_scales = keep.tile([P, T], U8, name="table_scales")
+        nc.vector.memset(table_scales[:].bitcast(I32), 0)
+        for q in range(4):
+            nc.sync.dma_start(
+                table_scales[32 * q : 32 * q + 4, :].bitcast(I32),
+                x_scales[0, 4 * q : 4 * q + 4, :].bitcast(I32),
+            )
+        w1_raw = [load_weight("w1_raw%d" % c, w1, c * HALF, HALF) for c in range(2)]
+        two_sb = load_list("two_sb", two)
+        n1_sb = load_list("n1_sb", n1)
+        w3_raw = load_weight("w3_raw", w3, 0, N)
+        n2_sb = load_list("n2_sb", n2)
+        gn_sb = keep.tile([P, PACK], F32, name="gn_sb")
+        nc.sync.dma_start(gn_sb[:], gn.rearrange("(p t) o -> p (t o)", t=PACK))
+        w2_raw = load_weight("w2_raw", w2, 0, N)
+        n3_sb = load_list("n3_sb", n3)
+
+        def pick_scales(name, lst, tag):
+            tile = keep.tile([P, S], U8, name=name, tag=tag, align_bytes=64)
+            nc.vector.tensor_copy(tile[:], table_scales[:].indirect(lst[:]))
+            return tile
+
+        def pick_words(name, lst):
+            tile = keep.tile([P, S], U32, name=name, align_bytes=64)
+            nc.vector.tensor_copy(tile[:], table_words[:].bitcast(U32).indirect(lst[:]))
+            return tile
+
+        xa_scales = pick_scales("xa_scales", offs_sb, "xa_scales")
+        xa_words = pick_words("xa_words", offs_sb)
+        xb_words = pick_words("xb_words", two_sb)
+
+        w1_bf = keep.tile([P, PACK, P, PACK], BF16, name="w1_bf", tag="w1_bf", align_bytes=64)
+        for c, copy in enumerate((nc.scalar.copy, nc.scalar.copy)):
+            copy(
+                w1_bf[:, :, c * 64 : (c + 1) * 64, :].rearrange("p t m j -> p m j t"),
+                w1_raw[c][:].rearrange("p j (m t) -> p m j t", t=PACK),
+            )
+        w1_words = keep.tile([P, H], U32, name="w1_words", align_bytes=64)
+        w1_scales = keep.tile([P, H], U8, name="w1_scales", align_bytes=64)
+        y_ps = []
+        for t in range(PACK):
+            cols = slice(t * P, (t + 1) * P)
+            nc.vector.quantize_mx(
+                out=w1_words[:, cols].bitcast(FP8X4),
+                scales=w1_scales[:, cols],
+                in_=w1_bf[:, t].rearrange("p m j -> p (m j)"),
+            )
+            bank = psum.tile([P, S], F32, name="y_ps%d" % t, tag="bank%d" % t)
+            nc.tensor.matmul_mx(
+                out=bank[:],
+                lhsT=w1_words[:, cols].bitcast(FP8X4),
+                lhsT_scale=w1_scales[:, cols],
+                rhs=xa_words[:].bitcast(FP8X4),
+                rhs_scale=xa_scales[:],
+                start=True,
+                stop=True,
+            )
+            y_ps.append(bank)
+
+        xb_scales = pick_scales("xb_scales", two_sb, "w1_bf")
+
+        def quantise_weight(name, raw):
+            grouped = keep.tile([P, N, PACK], BF16, name=name + "_bf", tag=name + "_bf", align_bytes=64)
+            words = keep.tile([P, N], U32, name=name + "_words", align_bytes=64)
+            scales = keep.tile([P, N], U8, name=name + "_scales", align_bytes=64)
+            for c in range(2):
+                cols = slice(c * HALF, (c + 1) * HALF)
+                nc.vector.tensor_copy(
+                    grouped[:, cols, :].rearrange("p (c i) j -> p c j i", i=4),
+                    raw[:, :, cols].rearrange("p j (c i) -> p c j i", i=4),
+                )
+            nc.vector.quantize_mx(
+                out=words[:].bitcast(FP8X4), scales=scales[:], in_=grouped[:].rearrange("p n j -> p (n j)")
+            )
+            return words, scales
+
+        w3_words, w3_scales = quantise_weight("w3", w3_raw)
+        w2_words, w2_scales = quantise_weight("w2", w2_raw)
+
+        st = []
+        for t in range(PACK):
+            y_sb = keep.tile([P, S], F32, name="y_sb%d" % t)
+            if t < PACK - 1:
+                nc.scalar.activation(y_sb[:], y_ps[t][:], ACT.Copy)
+            else:
+                nc.vector.tensor_copy(y_sb[:], y_ps[t][:])
+            y_n1 = keep.tile([P, S], F32, name="y_n1_%d" % t)
+            for c in range(2):
+                nc.scalar.activation(
+                    y_n1[:, c * HALF : (c + 1) * HALF], y_sb[:].indirect(entries(n1_sb, c * HALF, HALF)), ACT.Copy
+                )
+            st_t = keep.tile([P, S], F32, name="st%d" % t, tag=("w3_bf", "st1", "w2_bf", "st3")[t], align_bytes=64)
+            nc.vector.tensor_tensor(st_t[:], y_n1[:], y_sb[:], ALU.max)
+            st.append(st_t)
+
+        early = S - CHUNKS[-1]
+        h_early = [psum.tile([P, early], F32, name="h_early%d" % m, tag="bank%d" % (4 + m)) for m in range(N // P)]
+        h_late = [psum.tile([P, CHUNKS[-1]], F32, name="h_late%d" % m, tag="bank%d" % m) for m in range(N // P)]
+        h_sb = [keep.tile([P, S], F32, name="h_sb%d" % m) for m in range(N // P)]
+        c0 = 0
+        for c, width in enumerate(CHUNKS):
+            cols = slice(c0, c0 + width)
+            low = keep.tile([P, PACK, width], F32, name="low%d" % c)
+            for t in range(PACK):
+                st_n2 = keep.tile([P, width], F32, name="st_n2_%d_%d" % (c, t))
+                nc.scalar.activation(st_n2[:], st[t][:].indirect(entries(n2_sb, c0, width)), ACT.Copy)
+                nc.vector.tensor_tensor(low[:, t, :], st_n2[:], st[t][:, cols], ALU.min)
+            z_bf = keep.tile([P, width, PACK], BF16, name="z_bf%d" % c, align_bytes=64)
+            nc.vector.tensor_tensor(
+                z_bf[:].rearrange("p (c i) t -> p c t i", i=4),
+                low[:].rearrange("p t (c i) -> p c t i", i=4),
+                gn_sb[:].rearrange("p (c t i) -> p c t i", c=1, i=1).to_broadcast([P, width // 4, PACK, 4]),
+                ALU.mult,
+            )
+            z_words = keep.tile([P, width], U32, name="z_words%d" % c, align_bytes=64)
+            z_scales = keep.tile([P, width], U8, name="z_scales%d" % c, align_bytes=64)
+            nc.vector.quantize_mx(
+                out=z_words[:].bitcast(FP8X4), scales=z_scales[:], in_=z_bf[:].rearrange("p n t -> p (n t)")
+            )
+            for m in range(N // P):
+                rows = slice(m * P, (m + 1) * P)
+                acc = h_early[m][:, cols] if c0 < early else h_late[m][:]
+                nc.tensor.matmul_mx(
+                    out=acc,
+                    lhsT=w3_words[:, rows].bitcast(FP8X4),
+                    lhsT_scale=w3_scales[:, rows],
+                    rhs=xb_words[:, cols].bitcast(FP8X4),
+                    rhs_scale=xb_scales[:, cols],
+                    start=True,
+                    stop=False,
+                )
+                nc.tensor.matmul_mx(
+                    out=acc,
+                    lhsT=w2_words[:, rows].bitcast(FP8X4),
+                    lhsT_scale=w2_scales[:, rows],
+                    rhs=z_words[:].bitcast(FP8X4),
+                    rhs_scale=z_scales[:],
+                    start=False,
+                    stop=True,
+                )
+            c0 = c0 + width
+            if c0 == early:
+                for m in range(N // P):
+                    nc.scalar.activation(h_sb[m][:, :early], h_early[m][:], ACT.Sigmoid if m == 0 else ACT.Copy)
+        nc.scalar.activation(h_sb[0][:, early:], h_late[0][:], ACT.Sigmoid)
+        for m in range(1, N // P):
+            nc.vector.tensor_copy(h_sb[m][:, early:], h_late[m][:])
+
+        for start, width, bank in ((0, early, h_early[0]), (early, S - early, h_late[0])):
+            gate = keep.tile([P, width], F32, name="gate0_%d" % start)
+            nc.vector.tensor_copy(gate[:], h_sb[0][:].indirect(entries(n3_sb, start, width)))
+            res = keep.tile([P, width], F32, name="res0_%d" % start)
+            nc.vector.tensor_tensor(res[:], gate[:], bank[:], ALU.mult)
+            nc.sync.dma_start(out[0:P, start : start + width], res[:])
+        for m in range(1, N // P):
+            for c in range(2):
+                cols = slice(c * HALF, (c + 1) * HALF)
+                gate = keep.tile([P, HALF], F32, name="gate%d_%d" % (m, c))
+                nc.scalar.activation(gate[:], h_sb[m][:].indirect(entries(n3_sb, c * HALF, HALF)), ACT.Sigmoid)
+                res = keep.tile([P, HALF], F32, name="res%d_%d" % (m, c))
+                nc.vector.tensor_tensor(res[:], gate[:], h_sb[m][:, cols], ALU.mult)
+                nc.sync.dma_start(out[m * P : (m + 1) * P, cols], res[:])

@@ -39,126 +39,169 @@ def tile_picked_mixinhopmngate_none_p_kernel(
             return tile[:, start // GROUP : (start + count) // GROUP]
 
         def load_weight(name, dram, c0, width):
-            tile = keep.tile([P, PACK, width], F32, name=name)
+            tile = keep.tile([P, PACK, width], F32, name=name, tag=name, align_bytes=64)
             nc.sync.dma_start(tile[:], dram.rearrange("(p j) c -> p j c", j=PACK)[:, :, c0 : c0 + width])
             return tile
 
-        offs_sb = load_list("offs_sb", offs)
-        table_words = keep.tile([P, T], I32, name="table_words")
-        nc.sync.dma_start(table_words[:], x_words[0].rearrange("p n t -> p (n t)").bitcast(I32))
         table_scales = keep.tile([P, T], U8, name="table_scales")
-        nc.vector.memset(table_scales[:].bitcast(I32), 0)
+        nc.gpsimd.memset(table_scales[:, : T // 2].bitcast(I32), 0)
+        nc.vector.memset(table_scales[:, T // 2 :].bitcast(I32), 0)
+        warm = keep.tile([P, 2], F32, name="warm")
+        nc.vector.memset(warm[:, 0:1], 0.0)
+        nc.scalar.activation(warm[:, 1:2], warm[:, 0:1], ACT.Sigmoid)
+
+        offs_sb = load_list("offs_sb", offs)
+        w1_raw = [load_weight("w1_raw0", w1, 0, HALF)]
+        two_sb = load_list("two_sb", two)
+        gn_sb = keep.tile([P, PACK], F32, name="gn_sb")
+        nc.gpsimd.dma_start(gn_sb[:], gn.rearrange("(p t) o -> p (t o)", t=PACK))
         for q in range(4):
             nc.sync.dma_start(
                 table_scales[32 * q : 32 * q + 4, :].bitcast(I32),
                 x_scales[0, 4 * q : 4 * q + 4, :].bitcast(I32),
             )
-        w1_raw = [load_weight("w1_raw%d" % c, w1, c * HALF, HALF) for c in range(2)]
-        two_sb = load_list("two_sb", two)
+        w1_raw.append(load_weight("w1_raw1", w1, HALF, HALF))
+        table_words = keep.tile([P, T], I32, name="table_words")
+        nc.sync.dma_start(table_words[:], x_words[0].rearrange("p n t -> p (n t)").bitcast(I32))
         n1_sb = load_list("n1_sb", n1)
         w3_raw = load_weight("w3_raw", w3, 0, N)
         n2_sb = load_list("n2_sb", n2)
-        gn_sb = keep.tile([P, PACK], F32, name="gn_sb")
-        nc.sync.dma_start(gn_sb[:], gn.rearrange("(p t) o -> p (t o)", t=PACK))
         w2_raw = load_weight("w2_raw", w2, 0, N)
         n3_sb = load_list("n3_sb", n3)
 
-        def pick_scales(name, lst, tag):
-            tile = keep.tile([P, S], U8, name=name, tag=tag, align_bytes=64)
+        def pick_scales(name, lst):
+            tile = keep.tile([P, S], U8, name=name, align_bytes=64)
             nc.vector.tensor_copy(tile[:], table_scales[:].indirect(lst[:]))
             return tile
 
-        def pick_words(name, lst):
-            tile = keep.tile([P, S], U32, name=name, align_bytes=64)
-            nc.vector.tensor_copy(tile[:], table_words[:].bitcast(U32).indirect(lst[:]))
-            return tile
+        xa_scales = pick_scales("xa_scales", offs_sb)
+        xb_scales = pick_scales("xb_scales", two_sb)
 
-        xa_scales = pick_scales("xa_scales", offs_sb, "xa_scales")
-        xa_words = pick_words("xa_words", offs_sb)
-        xb_words = pick_words("xb_words", two_sb)
-
-        w1_bf = keep.tile([P, PACK, P, PACK], BF16, name="w1_bf", tag="w1_bf", align_bytes=64)
-        for c, copy in enumerate((nc.scalar.copy, nc.scalar.copy)):
-            copy(
+        w1_bf = keep.tile([P, PACK, P, PACK], BF16, name="w1_bf", align_bytes=64)
+        for c in range(2):
+            nc.scalar.copy(
                 w1_bf[:, :, c * 64 : (c + 1) * 64, :].rearrange("p t m j -> p m j t"),
                 w1_raw[c][:].rearrange("p j (m t) -> p m j t", t=PACK),
             )
         w1_words = keep.tile([P, H], U32, name="w1_words", align_bytes=64)
         w1_scales = keep.tile([P, H], U8, name="w1_scales", align_bytes=64)
+        nc.vector.quantize_mx(
+            out=w1_words[:].bitcast(FP8X4), scales=w1_scales[:], in_=w1_bf[:].rearrange("p t m j -> p (t m j)")
+        )
+        xa_words = []
+        for c in range(2):
+            tile = keep.tile([P, HALF], U32, name="xa_words%d" % c, align_bytes=64)
+            nc.vector.tensor_copy(tile[:], table_words[:].bitcast(U32).indirect(entries(offs_sb, c * HALF, HALF)))
+            xa_words.append(tile)
+
+        gn_sign = keep.tile([P, PACK], F32, name="gn_sign")
+        gn_abs = keep.tile([P, PACK], F32, name="gn_abs")
+        gn_pos = keep.tile([P, PACK], F32, name="gn_pos")
+        nc.gpsimd.tensor_scalar(gn_pos[:], gn_sb[:], 0.0, None, ALU.is_ge)
+        nc.gpsimd.tensor_scalar(gn_sign[:], gn_pos[:], 2.0, -1.0, ALU.mult, ALU.add)
+        nc.gpsimd.tensor_tensor(gn_abs[:], gn_sb[:], gn_sign[:], ALU.mult)
+
         y_ps = []
         for t in range(PACK):
-            cols = slice(t * P, (t + 1) * P)
-            nc.vector.quantize_mx(
-                out=w1_words[:, cols].bitcast(FP8X4),
-                scales=w1_scales[:, cols],
-                in_=w1_bf[:, t].rearrange("p m j -> p (m j)"),
-            )
+            rows = slice(t * P, (t + 1) * P)
             bank = psum.tile([P, S], F32, name="y_ps%d" % t, tag="bank%d" % t)
-            nc.tensor.matmul_mx(
-                out=bank[:],
-                lhsT=w1_words[:, cols].bitcast(FP8X4),
-                lhsT_scale=w1_scales[:, cols],
-                rhs=xa_words[:].bitcast(FP8X4),
-                rhs_scale=xa_scales[:],
-                start=True,
-                stop=True,
-            )
+            for c in range(2):
+                cols = slice(c * HALF, (c + 1) * HALF)
+                nc.tensor.matmul_mx(
+                    out=bank[:, cols],
+                    lhsT=w1_words[:, rows].bitcast(FP8X4),
+                    lhsT_scale=w1_scales[:, rows],
+                    rhs=xa_words[c][:].bitcast(FP8X4),
+                    rhs_scale=xa_scales[:, cols],
+                    start=True,
+                    stop=True,
+                )
             y_ps.append(bank)
 
-        xb_scales = pick_scales("xb_scales", two_sb, "w1_bf")
+        xb_words = keep.tile([P, S], U32, name="xb_words", align_bytes=64)
+        nc.vector.tensor_copy(xb_words[:], table_words[:].bitcast(U32).indirect(two_sb[:]))
 
-        def quantise_weight(name, raw):
+        def quantise_weight(name, raw, row_sign):
             grouped = keep.tile([P, N, PACK], BF16, name=name + "_bf", tag=name + "_bf", align_bytes=64)
             words = keep.tile([P, N], U32, name=name + "_words", align_bytes=64)
             scales = keep.tile([P, N], U8, name=name + "_scales", align_bytes=64)
             for c in range(2):
                 cols = slice(c * HALF, (c + 1) * HALF)
-                nc.vector.tensor_copy(
-                    grouped[:, cols, :].rearrange("p (c i) j -> p c j i", i=4),
-                    raw[:, :, cols].rearrange("p j (c i) -> p c j i", i=4),
-                )
+                dst = grouped[:, cols, :].rearrange("p (c i) j -> p c j i", i=4)
+                src = raw[:, :, cols].rearrange("p j (c i) -> p c j i", i=4)
+                if row_sign is None:
+                    nc.vector.tensor_copy(dst, src)
+                else:
+                    sign = row_sign[:].rearrange("p (c j i) -> p c j i", c=1, i=1)
+                    nc.vector.tensor_tensor(dst, src, sign.to_broadcast([P, HALF // 4, PACK, 4]), ALU.mult)
             nc.vector.quantize_mx(
                 out=words[:].bitcast(FP8X4), scales=scales[:], in_=grouped[:].rearrange("p n j -> p (n j)")
             )
             return words, scales
 
-        w3_words, w3_scales = quantise_weight("w3", w3_raw)
-        w2_words, w2_scales = quantise_weight("w2", w2_raw)
+        w3_words, w3_scales = quantise_weight("w3", w3_raw, None)
+        w2_words, w2_scales = quantise_weight("w2", w2_raw, gn_sign)
 
         st = []
+        st_all = keep.tile([P, PACK, S], F32, name="st_all")
         for t in range(PACK):
-            y_sb = keep.tile([P, S], F32, name="y_sb%d" % t)
-            if t < PACK - 1:
-                nc.scalar.activation(y_sb[:], y_ps[t][:], ACT.Copy)
-            else:
-                nc.vector.tensor_copy(y_sb[:], y_ps[t][:])
-            y_n1 = keep.tile([P, S], F32, name="y_n1_%d" % t)
+            y_sb = keep.tile([P, S], F32, name="y_sb%d" % t, tag="y_sb%d" % t, align_bytes=64)
+            nc.scalar.activation(y_sb[:], y_ps[t][:], ACT.Copy, scale=gn_abs[:, t : t + 1])
+            y_n1 = keep.tile([P, S], F32, name="y_n1_%d" % t, tag="y_n1_%d" % t, align_bytes=64)
             for c in range(2):
                 nc.scalar.activation(
                     y_n1[:, c * HALF : (c + 1) * HALF], y_sb[:].indirect(entries(n1_sb, c * HALF, HALF)), ACT.Copy
                 )
-            st_t = keep.tile([P, S], F32, name="st%d" % t, tag=("w3_bf", "st1", "w2_bf", "st3")[t], align_bytes=64)
+            st_t = keep.tile([P, S], F32, name="st%d" % t, tag=("w3_bf", "w2_raw", "y_n1_1", "w2_bf")[t], align_bytes=64)
             nc.vector.tensor_tensor(st_t[:], y_n1[:], y_sb[:], ALU.max)
+            if t < PACK - 1:
+                nc.sync.dma_start(st_all[:, t, :], st_t[:])
+            else:
+                nc.vector.tensor_copy(st_all[:, t, :], st_t[:])
             st.append(st_t)
 
-        early = S - CHUNKS[-1]
+        early = CHUNKS[0]
         h_early = [psum.tile([P, early], F32, name="h_early%d" % m, tag="bank%d" % (4 + m)) for m in range(N // P)]
-        h_late = [psum.tile([P, CHUNKS[-1]], F32, name="h_late%d" % m, tag="bank%d" % m) for m in range(N // P)]
+        h_late = [psum.tile([P, S - early], F32, name="h_late%d" % m, tag="bank%d" % m) for m in range(N // P)]
         h_sb = [keep.tile([P, S], F32, name="h_sb%d" % m) for m in range(N // P)]
+        starts = [sum(CHUNKS[:c]) for c in range(len(CHUNKS))]
+
+        def h_acc(m, c):
+            if starts[c] < early:
+                return h_early[m][:]
+            return h_late[m][:, starts[c] - early : starts[c] - early + CHUNKS[c]]
+
+        for c, width in enumerate(CHUNKS):
+            cols = slice(starts[c], starts[c] + width)
+            for m in range(N // P):
+                rows = slice(m * P, (m + 1) * P)
+                nc.tensor.matmul_mx(
+                    out=h_acc(m, c),
+                    lhsT=w3_words[:, rows].bitcast(FP8X4),
+                    lhsT_scale=w3_scales[:, rows],
+                    rhs=xb_words[:, cols].bitcast(FP8X4),
+                    rhs_scale=xb_scales[:, cols],
+                    start=starts[c] in (0, early),
+                    stop=False,
+                )
         c0 = 0
         for c, width in enumerate(CHUNKS):
             cols = slice(c0, c0 + width)
-            low = keep.tile([P, PACK, width], F32, name="low%d" % c)
+            st_n2 = keep.tile(
+                [P, PACK, width], F32, name="st_n2_%d" % c, tag=("st_n2", "y_sb3", "y_n1_3")[c], align_bytes=64
+            )
             for t in range(PACK):
-                st_n2 = keep.tile([P, width], F32, name="st_n2_%d_%d" % (c, t))
-                nc.scalar.activation(st_n2[:], st[t][:].indirect(entries(n2_sb, c0, width)), ACT.Copy)
-                nc.vector.tensor_tensor(low[:, t, :], st_n2[:], st[t][:, cols], ALU.min)
+                window = st[t][:].indirect(entries(n2_sb, c0, width))
+                if t < PACK - 1 or c > 0:
+                    nc.scalar.activation(st_n2[:, t, :], window, ACT.Copy)
+                else:
+                    nc.vector.tensor_copy(st_n2[:, t, :], window)
             z_bf = keep.tile([P, width, PACK], BF16, name="z_bf%d" % c, align_bytes=64)
             nc.vector.tensor_tensor(
                 z_bf[:].rearrange("p (c i) t -> p c t i", i=4),
-                low[:].rearrange("p t (c i) -> p c t i", i=4),
-                gn_sb[:].rearrange("p (c t i) -> p c t i", c=1, i=1).to_broadcast([P, width // 4, PACK, 4]),
-                ALU.mult,
+                st_n2[:].rearrange("p t (c i) -> p c t i", i=4),
+                st_all[:, :, cols].rearrange("p t (c i) -> p c t i", i=4),
+                ALU.min,
             )
             z_words = keep.tile([P, width], U32, name="z_words%d" % c, align_bytes=64)
             z_scales = keep.tile([P, width], U8, name="z_scales%d" % c, align_bytes=64)
@@ -167,24 +210,14 @@ def tile_picked_mixinhopmngate_none_p_kernel(
             )
             for m in range(N // P):
                 rows = slice(m * P, (m + 1) * P)
-                acc = h_early[m][:, cols] if c0 < early else h_late[m][:]
                 nc.tensor.matmul_mx(
-                    out=acc,
-                    lhsT=w3_words[:, rows].bitcast(FP8X4),
-                    lhsT_scale=w3_scales[:, rows],
-                    rhs=xb_words[:, cols].bitcast(FP8X4),
-                    rhs_scale=xb_scales[:, cols],
-                    start=True,
-                    stop=False,
-                )
-                nc.tensor.matmul_mx(
-                    out=acc,
+                    out=h_acc(m, c),
                     lhsT=w2_words[:, rows].bitcast(FP8X4),
                     lhsT_scale=w2_scales[:, rows],
                     rhs=z_words[:].bitcast(FP8X4),
                     rhs_scale=z_scales[:],
                     start=False,
-                    stop=True,
+                    stop=c0 + width in (early, S),
                 )
             c0 = c0 + width
             if c0 == early:

@@ -66,7 +66,7 @@ def tile_picked_mixinhopmngate_none_p_kernel(
         n1_sb = load_list("n1_sb", n1)
         w3_raw = load_weight("w3_raw", w3, 0, N)
         n2_sb = load_list("n2_sb", n2)
-        w2_raw = load_weight("w2_raw", w2, 0, N)
+        w2_raw = [load_weight("w2_raw%d" % c, w2, c * HALF, HALF) for c in range(2)]
         n3_sb = load_list("n3_sb", n3)
 
         def pick_scales(name, lst):
@@ -121,26 +121,29 @@ def tile_picked_mixinhopmngate_none_p_kernel(
         xb_words = keep.tile([P, S], U32, name="xb_words", align_bytes=64)
         nc.vector.tensor_copy(xb_words[:], table_words[:].bitcast(U32).indirect(two_sb[:]))
 
-        def quantise_weight(name, raw, row_sign):
-            grouped = keep.tile([P, N, PACK], BF16, name=name + "_bf", tag=name + "_bf", align_bytes=64)
-            words = keep.tile([P, N], U32, name=name + "_words", align_bytes=64)
-            scales = keep.tile([P, N], U8, name=name + "_scales", align_bytes=64)
-            for c in range(2):
-                cols = slice(c * HALF, (c + 1) * HALF)
-                dst = grouped[:, cols, :].rearrange("p (c i) j -> p c j i", i=4)
-                src = raw[:, :, cols].rearrange("p j (c i) -> p c j i", i=4)
-                if row_sign is None:
-                    nc.vector.tensor_copy(dst, src)
-                else:
-                    sign = row_sign[:].rearrange("p (c j i) -> p c j i", c=1, i=1)
-                    nc.vector.tensor_tensor(dst, src, sign.to_broadcast([P, HALF // 4, PACK, 4]), ALU.mult)
+        def quantise(name, grouped):
+            width = grouped.shape[1]
+            words = keep.tile([P, width], U32, name=name + "_words", align_bytes=64)
+            scales = keep.tile([P, width], U8, name=name + "_scales", align_bytes=64)
             nc.vector.quantize_mx(
                 out=words[:].bitcast(FP8X4), scales=scales[:], in_=grouped[:].rearrange("p n j -> p (n j)")
             )
             return words, scales
 
-        w3_words, w3_scales = quantise_weight("w3", w3_raw, None)
-        w2_words, w2_scales = quantise_weight("w2", w2_raw, gn_sign)
+        w3_bf = keep.tile([P, N, PACK], BF16, name="w3_bf", tag="w3_bf", align_bytes=64)
+        for c in range(4):
+            cols = slice(c * P, (c + 1) * P)
+            nc.gpsimd.tensor_scalar(
+                w3_bf[:, cols, :], w3_raw[:, :, cols].rearrange("p j n -> p n j"), 1.0, 0.0, ALU.mult, ALU.add
+            )
+        w2_bf = keep.tile([P, N, PACK], BF16, name="w2_bf", tag="w2_bf", align_bytes=64)
+        for c in range(2):
+            nc.gpsimd.tensor_tensor(
+                w2_bf[:, c * P : (c + 1) * P, :],
+                w2_raw[0][:, :, c * P : (c + 1) * P].rearrange("p j n -> p n j"),
+                gn_sign[:].rearrange("p (n j) -> p n j", n=1).to_broadcast([P, P, PACK]),
+                ALU.mult,
+            )
 
         st = []
         st_all = keep.tile([P, PACK, S], F32, name="st_all")
@@ -149,16 +152,28 @@ def tile_picked_mixinhopmngate_none_p_kernel(
             nc.scalar.activation(y_sb[:], y_ps[t][:], ACT.Copy, scale=gn_abs[:, t : t + 1])
             y_n1 = keep.tile([P, S], F32, name="y_n1_%d" % t, tag="y_n1_%d" % t, align_bytes=64)
             for c in range(2):
-                nc.scalar.activation(
-                    y_n1[:, c * HALF : (c + 1) * HALF], y_sb[:].indirect(entries(n1_sb, c * HALF, HALF)), ACT.Copy
+                window = y_sb[:].indirect(entries(n1_sb, c * HALF, HALF))
+                if t == 1:
+                    nc.vector.tensor_copy(y_n1[:, c * HALF : (c + 1) * HALF], window)
+                else:
+                    nc.scalar.activation(y_n1[:, c * HALF : (c + 1) * HALF], window, ACT.Copy)
+            st_t = keep.tile([P, S], F32, name="st%d" % t)
+            nc.vector.scalar_tensor_tensor(st_t[:], y_ps[t][:], gn_abs[:, t : t + 1], y_n1[:], ALU.mult, ALU.max)
+            if t == 1:
+                nc.vector.tensor_tensor(
+                    w2_bf[:, HALF:, :].rearrange("p (c i) j -> p c j i", i=4),
+                    w2_raw[1][:].rearrange("p j (c i) -> p c j i", i=4),
+                    gn_sign[:].rearrange("p (c j i) -> p c j i", c=1, i=1).to_broadcast([P, HALF // 4, PACK, 4]),
+                    ALU.mult,
                 )
-            st_t = keep.tile([P, S], F32, name="st%d" % t, tag=("w3_bf", "w2_raw", "y_n1_1", "w2_bf")[t], align_bytes=64)
-            nc.vector.tensor_tensor(st_t[:], y_n1[:], y_sb[:], ALU.max)
+            if t == 2:
+                w3_words, w3_scales = quantise("w3", w3_bf)
             if t < PACK - 1:
                 nc.sync.dma_start(st_all[:, t, :], st_t[:])
             else:
                 nc.vector.tensor_copy(st_all[:, t, :], st_t[:])
             st.append(st_t)
+        w2_words, w2_scales = quantise("w2", w2_bf)
 
         early = CHUNKS[0]
         h_early = [psum.tile([P, early], F32, name="h_early%d" % m, tag="bank%d" % (4 + m)) for m in range(N // P)]
@@ -192,22 +207,18 @@ def tile_picked_mixinhopmngate_none_p_kernel(
             )
             for t in range(PACK):
                 window = st[t][:].indirect(entries(n2_sb, c0, width))
-                if t < PACK - 1 or c > 0:
+                if t < PACK - 1 or c > 1:
                     nc.scalar.activation(st_n2[:, t, :], window, ACT.Copy)
                 else:
                     nc.vector.tensor_copy(st_n2[:, t, :], window)
-            z_bf = keep.tile([P, width, PACK], BF16, name="z_bf%d" % c, align_bytes=64)
+            z_bf = keep.tile([P, width, PACK], BF16, name="z_bf%d" % c, tag=("w2_bf", "z_bf1", "z_bf2")[c], align_bytes=64)
             nc.vector.tensor_tensor(
                 z_bf[:].rearrange("p (c i) t -> p c t i", i=4),
                 st_n2[:].rearrange("p t (c i) -> p c t i", i=4),
                 st_all[:, :, cols].rearrange("p t (c i) -> p c t i", i=4),
                 ALU.min,
             )
-            z_words = keep.tile([P, width], U32, name="z_words%d" % c, align_bytes=64)
-            z_scales = keep.tile([P, width], U8, name="z_scales%d" % c, align_bytes=64)
-            nc.vector.quantize_mx(
-                out=z_words[:].bitcast(FP8X4), scales=z_scales[:], in_=z_bf[:].rearrange("p n t -> p (n t)")
-            )
+            z_words, z_scales = quantise("z%d" % c, z_bf)
             for m in range(N // P):
                 rows = slice(m * P, (m + 1) * P)
                 nc.tensor.matmul_mx(

from contextlib import ExitStack

import concourse.mybir as mybir

K, T, S, N, H = 512, 2048, 512, 512, 512
FLOPS = 2 * S * (K * H + H * N + K * N)

F32 = mybir.dt.float32
BF16 = mybir.dt.bfloat16
I32 = mybir.dt.int32
U32 = mybir.dt.uint32
U16 = mybir.dt.uint16
U8 = mybir.dt.uint8
FP8X4 = mybir.dt.float8_e4m3fn_x4
ALU = mybir.AluOpType
ACT = mybir.ActivationFunctionType

P = 128
PACK = 4
GROUP = 16
HALF = S // 2
CHUNKS = (256, 128, 128)


def tile_picked_mixinhopmngate_none_p_kernel(
    tc, x_words, x_scales, w1, gn, w2, w3, offs, n1, n2, two, n3, out
):
    nc = tc.nc
    with ExitStack() as ctx:
        keep = ctx.enter_context(tc.tile_pool(name="keep", bufs=1))
        psum = ctx.enter_context(tc.psum_pool(name="psum", bufs=1))

        def load_list(name, dram):
            tile = keep.tile([P, S // GROUP], U16, name=name)
            nc.sync.dma_start(tile[:], dram)
            return tile

        def entries(tile, start, count):
            return tile[:, start // GROUP : (start + count) // GROUP]

        def load_weight(name, dram, c0, width):
            tile = keep.tile([P, PACK, width], F32, name=name, tag=name, align_bytes=64)
            nc.sync.dma_start(tile[:], dram.rearrange("(p j) c -> p j c", j=PACK)[:, :, c0 : c0 + width])
            return tile

        table_scales = keep.tile([P, T], U8, name="table_scales")
        nc.gpsimd.memset(table_scales[:, : T // 2].bitcast(I32), 0)
        nc.vector.memset(table_scales[:, T // 2 :].bitcast(I32), 0)
        warm = keep.tile([P, 2], F32, name="warm")
        nc.vector.memset(warm[:, 0:1], 0.0)
        nc.scalar.activation(warm[:, 1:2], warm[:, 0:1], ACT.Sigmoid)

        offs_sb = load_list("offs_sb", offs)
        w1_raw = [load_weight("w1_raw0", w1, 0, HALF)]
        two_sb = load_list("two_sb", two)
        gn_sb = keep.tile([P, PACK], F32, name="gn_sb")
        nc.gpsimd.dma_start(gn_sb[:], gn.rearrange("(p t) o -> p (t o)", t=PACK))
        for q in range(4):
            nc.sync.dma_start(
                table_scales[32 * q : 32 * q + 4, :].bitcast(I32),
                x_scales[0, 4 * q : 4 * q + 4, :].bitcast(I32),
            )
        w1_raw.append(load_weight("w1_raw1", w1, HALF, HALF))
        table_words = keep.tile([P, T], I32, name="table_words")
        nc.sync.dma_start(table_words[:], x_words[0].rearrange("p n t -> p (n t)").bitcast(I32))
        n1_sb = load_list("n1_sb", n1)
        w3_raw = load_weight("w3_raw", w3, 0, N)
        n2_sb = load_list("n2_sb", n2)
        w2_raw = [load_weight("w2_raw%d" % c, w2, c * HALF, HALF) for c in range(2)]
        n3_sb = load_list("n3_sb", n3)

        def pick_scales(name, lst):
            tile = keep.tile([P, S], U8, name=name, align_bytes=64)
            nc.vector.tensor_copy(tile[:], table_scales[:].indirect(lst[:]))
            return tile

        xa_scales = pick_scales("xa_scales", offs_sb)
        xb_scales = pick_scales("xb_scales", two_sb)

        w1_bf = keep.tile([P, PACK, P, PACK], BF16, name="w1_bf", align_bytes=64)
        for c in range(2):
            nc.scalar.copy(
                w1_bf[:, :, c * 64 : (c + 1) * 64, :].rearrange("p t m j -> p m j t"),
                w1_raw[c][:].rearrange("p j (m t) -> p m j t", t=PACK),
            )
        w1_words = keep.tile([P, H], U32, name="w1_words", align_bytes=64)
        w1_scales = keep.tile([P, H], U8, name="w1_scales", align_bytes=64)
        nc.vector.quantize_mx(
            out=w1_words[:].bitcast(FP8X4), scales=w1_scales[:], in_=w1_bf[:].rearrange("p t m j -> p (t m j)")
        )
        xa_words = []
        for c in range(2):
            tile = keep.tile([P, HALF], U32, name="xa_words%d" % c, align_bytes=64)
            nc.vector.tensor_copy(tile[:], table_words[:].bitcast(U32).indirect(entries(offs_sb, c * HALF, HALF)))
            xa_words.append(tile)

        gn_sign = keep.tile([P, PACK], F32, name="gn_sign")
        gn_abs = keep.tile([P, PACK], F32, name="gn_abs")
        gn_pos = keep.tile([P, PACK], F32, name="gn_pos")
        nc.gpsimd.tensor_scalar(gn_pos[:], gn_sb[:], 0.0, None, ALU.is_ge)
        nc.gpsimd.tensor_scalar(gn_sign[:], gn_pos[:], 2.0, -1.0, ALU.mult, ALU.add)
        nc.gpsimd.tensor_tensor(gn_abs[:], gn_sb[:], gn_sign[:], ALU.mult)

        y_ps = []
        for t in range(PACK):
            rows = slice(t * P, (t + 1) * P)
            bank = psum.tile([P, S], F32, name="y_ps%d" % t, tag="bank%d" % t)
            for c in range(2):
                cols = slice(c * HALF, (c + 1) * HALF)
                nc.tensor.matmul_mx(
                    out=bank[:, cols],
                    lhsT=w1_words[:, rows].bitcast(FP8X4),
                    lhsT_scale=w1_scales[:, rows],
                    rhs=xa_words[c][:].bitcast(FP8X4),
                    rhs_scale=xa_scales[:, cols],
                    start=True,
                    stop=True,
                )
            y_ps.append(bank)

        xb_words = keep.tile([P, S], U32, name="xb_words", align_bytes=64)
        nc.vector.tensor_copy(xb_words[:], table_words[:].bitcast(U32).indirect(two_sb[:]))

        def quantise(name, grouped):
            width = grouped.shape[1]
            words = keep.tile([P, width], U32, name=name + "_words", align_bytes=64)
            scales = keep.tile([P, width], U8, name=name + "_scales", align_bytes=64)
            nc.vector.quantize_mx(
                out=words[:].bitcast(FP8X4), scales=scales[:], in_=grouped[:].rearrange("p n j -> p (n j)")
            )
            return words, scales

        w3_bf = keep.tile([P, N, PACK], BF16, name="w3_bf", tag="w3_bf", align_bytes=64)
        for c in range(4):
            cols = slice(c * P, (c + 1) * P)
            nc.gpsimd.tensor_scalar(
                w3_bf[:, cols, :], w3_raw[:, :, cols].rearrange("p j n -> p n j"), 1.0, 0.0, ALU.mult, ALU.add
            )
        w2_bf = keep.tile([P, N, PACK], BF16, name="w2_bf", tag="w2_bf", align_bytes=64)
        for c in range(2):
            nc.gpsimd.tensor_tensor(
                w2_bf[:, c * P : (c + 1) * P, :],
                w2_raw[0][:, :, c * P : (c + 1) * P].rearrange("p j n -> p n j"),
                gn_sign[:].rearrange("p (n j) -> p n j", n=1).to_broadcast([P, P, PACK]),
                ALU.mult,
            )

        st = []
        st_all = keep.tile([P, PACK, S], F32, name="st_all")
        for t in range(PACK):
            y_sb = keep.tile([P, S], F32, name="y_sb%d" % t, tag="y_sb%d" % t, align_bytes=64)
            nc.scalar.activation(y_sb[:], y_ps[t][:], ACT.Copy, scale=gn_abs[:, t : t + 1])
            y_n1 = keep.tile([P, S], F32, name="y_n1_%d" % t, tag="y_n1_%d" % t, align_bytes=64)
            for c in range(2):
                window = y_sb[:].indirect(entries(n1_sb, c * HALF, HALF))
                if t == 1:
                    nc.vector.tensor_copy(y_n1[:, c * HALF : (c + 1) * HALF], window)
                else:
                    nc.scalar.activation(y_n1[:, c * HALF : (c + 1) * HALF], window, ACT.Copy)
            st_t = keep.tile([P, S], F32, name="st%d" % t)
            nc.vector.scalar_tensor_tensor(st_t[:], y_ps[t][:], gn_abs[:, t : t + 1], y_n1[:], ALU.mult, ALU.max)
            if t == 1:
                nc.vector.tensor_tensor(
                    w2_bf[:, HALF:, :].rearrange("p (c i) j -> p c j i", i=4),
                    w2_raw[1][:].rearrange("p j (c i) -> p c j i", i=4),
                    gn_sign[:].rearrange("p (c j i) -> p c j i", c=1, i=1).to_broadcast([P, HALF // 4, PACK, 4]),
                    ALU.mult,
                )
            if t == 2:
                w3_words, w3_scales = quantise("w3", w3_bf)
            if t < PACK - 1:
                nc.sync.dma_start(st_all[:, t, :], st_t[:])
            else:
                nc.vector.tensor_copy(st_all[:, t, :], st_t[:])
            st.append(st_t)
        w2_words, w2_scales = quantise("w2", w2_bf)

        early = CHUNKS[0]
        h_early = [psum.tile([P, early], F32, name="h_early%d" % m, tag="bank%d" % (4 + m)) for m in range(N // P)]
        h_late = [psum.tile([P, S - early], F32, name="h_late%d" % m, tag="bank%d" % m) for m in range(N // P)]
        h_sb = [keep.tile([P, S], F32, name="h_sb%d" % m) for m in range(N // P)]
        starts = [sum(CHUNKS[:c]) for c in range(len(CHUNKS))]

        def h_acc(m, c):
            if starts[c] < early:
                return h_early[m][:]
            return h_late[m][:, starts[c] - early : starts[c] - early + CHUNKS[c]]

        for c, width in enumerate(CHUNKS):
            cols = slice(starts[c], starts[c] + width)
            for m in range(N // P):
                rows = slice(m * P, (m + 1) * P)
                nc.tensor.matmul_mx(
                    out=h_acc(m, c),
                    lhsT=w3_words[:, rows].bitcast(FP8X4),
                    lhsT_scale=w3_scales[:, rows],
                    rhs=xb_words[:, cols].bitcast(FP8X4),
                    rhs_scale=xb_scales[:, cols],
                    start=starts[c] in (0, early),
                    stop=False,
                )
        c0 = 0
        for c, width in enumerate(CHUNKS):
            cols = slice(c0, c0 + width)
            st_n2 = keep.tile(
                [P, PACK, width], F32, name="st_n2_%d" % c, tag=("st_n2", "y_sb3", "y_n1_3")[c], align_bytes=64
            )
            for t in range(PACK):
                window = st[t][:].indirect(entries(n2_sb, c0, width))
                if t < PACK - 1 or c > 1:
                    nc.scalar.activation(st_n2[:, t, :], window, ACT.Copy)
                else:
                    nc.vector.tensor_copy(st_n2[:, t, :], window)
            z_bf = keep.tile([P, width, PACK], BF16, name="z_bf%d" % c, tag=("w2_bf", "z_bf1", "z_bf2")[c], align_bytes=64)
            nc.vector.tensor_tensor(
                z_bf[:].rearrange("p (c i) t -> p c t i", i=4),
                st_n2[:].rearrange("p t (c i) -> p c t i", i=4),
                st_all[:, :, cols].rearrange("p t (c i) -> p c t i", i=4),
                ALU.min,
            )
            z_words, z_scales = quantise("z%d" % c, z_bf)
            for m in range(N // P):
                rows = slice(m * P, (m + 1) * P)
                nc.tensor.matmul_mx(
                    out=h_acc(m, c),
                    lhsT=w2_words[:, rows].bitcast(FP8X4),
                    lhsT_scale=w2_scales[:, rows],
                    rhs=z_words[:].bitcast(FP8X4),
                    rhs_scale=z_scales[:],
                    start=False,
                    stop=c0 + width in (early, S),
                )
            c0 = c0 + width
            if c0 == early:
                for m in range(N // P):
                    nc.scalar.activation(h_sb[m][:, :early], h_early[m][:], ACT.Sigmoid if m == 0 else ACT.Copy)
        nc.scalar.activation(h_sb[0][:, early:], h_late[0][:], ACT.Sigmoid)
        for m in range(1, N // P):
            nc.vector.tensor_copy(h_sb[m][:, early:], h_late[m][:])

        for start, width, bank in ((0, early, h_early[0]), (early, S - early, h_late[0])):
            gate = keep.tile([P, width], F32, name="gate0_%d" % start)
            nc.vector.tensor_copy(gate[:], h_sb[0][:].indirect(entries(n3_sb, start, width)))
            res = keep.tile([P, width], F32, name="res0_%d" % start)
            nc.vector.tensor_tensor(res[:], gate[:], bank[:], ALU.mult)
            nc.sync.dma_start(out[0:P, start : start + width], res[:])
        for m in range(1, N // P):
            for c in range(2):
                cols = slice(c * HALF, (c + 1) * HALF)
                gate = keep.tile([P, HALF], F32, name="gate%d_%d" % (m, c))
                nc.scalar.activation(gate[:], h_sb[m][:].indirect(entries(n3_sb, c * HALF, HALF)), ACT.Sigmoid)
                res = keep.tile([P, HALF], F32, name="res%d_%d" % (m, c))
                nc.vector.tensor_tensor(res[:], gate[:], h_sb[m][:, cols], ALU.mult)
                nc.sync.dma_start(out[m * P : (m + 1) * P, cols], res[:])
